import numpy as np
CORES = [33,161,289,417,57,185,313,441]
N = 8
TK = 256
D = 128 * N
EPS = 0.01
def setup_inputs(rng):
    return {"x": (rng.standard_normal((N, 128, TK), dtype=np.float32) * (0.5 + np.abs(rng.standard_normal((1, 1, TK), dtype=np.float32))) + rng.standard_normal((1, 1, TK), dtype=np.float32)), "w": (rng.standard_normal((N, 128, 128), dtype=np.float32) / 11)}
def setup_inputs_big(rng):
    d = setup_inputs(rng)
    for k in ("x", "w"): d[k] = (d[k].astype(np.float32) * 1048576.0).astype(d[k].dtype)
    return d
def setup_inputs_small(rng):
    d = setup_inputs(rng)
    for k in ("x", "w"): d[k] = (d[k].astype(np.float32) * (1 / 1048576.0)).astype(d[k].dtype)
    return d
def setup_inputs_apart(rng):
    d = setup_inputs(rng)
    f = (10.0 ** rng.permutation(np.linspace(-1.5, 1.5, N))).astype(np.float32).reshape(N, 1, 1)
    for k in ("x", "w"): d[k] = (d[k].astype(np.float32) * f).astype(d[k].dtype)
    return d
def setup_inputs_mixed(rng):
    d = setup_inputs(rng)
    f = (10.0 ** rng.uniform(-3, 3, (1, 1, TK))).astype(np.float32); shape = rng.integers(3, size=(1, 1, TK))
    for k in ("x",):
        x = d[k].astype(np.float32)
        m = x.mean(axis=(0, 1), keepdims=True); level = m + np.sign(x - m) * np.abs(x - m).mean(axis=(0, 1), keepdims=True) * rng.uniform(0.9, 1.1, x.shape).astype(np.float32)
        other = x * np.where(rng.random(x.shape) < 0.5, 0.1, 1.0).astype(np.float32)
        d[k] = (np.where(shape == 1, level, np.where(shape == 2, other, x)) * f).astype(d[k].dtype)
    return d
def reference(x, w):
    X = x.astype(np.float64)
    Z = X
    Z = Z / np.sqrt((Z ** 2).sum(axis=(0, 1)) / D + EPS)
    s = sum(w[r].astype(np.float64).T @ Z[r] for r in range(N)).astype(np.float32)
    return {"y": np.broadcast_to(s, (N,) + s.shape)}

@@ -1,0 +1,220 @@
+from concourse.bass import DstId, RemoteDMATransfer
+from concourse.mybir import AluOpType, ActivationFunctionType
+
+N = 8
+H = 128
+D = 128 * N
+EPS = 0.01
+
+SCRATCH = {
+    "xs": ("sbuf", [128, 2 * H], "float32"),
+    "ws": ("sbuf", [128, H], "float32"),
+    "sq": ("sbuf", [128, 2 * H], "float32"),
+    "ones": ("sbuf", [128, H], "float32"),
+    "ident": ("sbuf", [128, H], "float32"),
+    "pbuf": ("sbuf", [128, 2 * H], "float32"),
+    "sown": ("sbuf", [128, 2], "float32"),
+    "fa": ("sbuf", [128, H], "float32"),
+    "fb": ("sbuf", [128, H], "float32"),
+    "sfa": ("sbuf", [128, 2], "float32"),
+    "sfb": ("sbuf", [128, 2], "float32"),
+    "sland": ("sbuf", [128, 8], "float32"),
+    "land0": ("sbuf", [128, 4 * H], "float32"),
+    "land1": ("sbuf", [128, 4 * H], "float32"),
+    "s4": ("sbuf", [128, 4], "float32"),
+    "s2": ("sbuf", [128, 2], "float32"),
+    "rt": ("sbuf", [128, 2], "float32"),
+    "rs": ("sbuf", [128, 2], "float32"),
+    "diag": ("sbuf", [128, 2 * H], "float32"),
+    "tb": ("sbuf", [128, 2 * H], "float32"),
+    "yb": ("sbuf", [128, 2 * H], "float32"),
+    "pp0": ("psum", [128, 512], "float32"),
+    "pp1": ("psum", [128, 512], "float32"),
+    "ps": ("psum", [128, 512], "float32"),
+    "pb0": ("psum", [128, 512], "float32"),
+    "pb1": ("psum", [128, 512], "float32"),
+    "pa0": ("psum", [128, 512], "float32"),
+    "pa1": ("psum", [128, 512], "float32"),
+}
+SEMAPHORES = (["ldx", "ldw", "c1", "cid", "sqd", "mm0", "mms", "mm1", "cp", "cps", "lsem", "feed", "sfeed", "sarr",
+               "v1", "v2", "a1", "v3", "v4", "b0", "b1", "acc0", "acc1", "yd0", "yd1", "st0", "st1"]
+              + ["arr%d_%d" % (k, j) for k in range(4) for j in range(2)])
+
+
+def _bits(m):
+    return [i for i in range(m.bit_length()) if (m >> i) & 1]
+
+
+def _mk(bits):
+    return sum(1 << i for i in bits)
+
+
+def _plan(T, topo):
+    ranks = list(T.cores)
+    info, role = {}, {}
+    n = topo.CORES_PER_CHIP
+    for c in ranks:
+        chip = [d for d in range(max(0, c - n + 1), c + n)
+                if topo.host(d) == topo.host(c) and topo.chip(d) == topo.chip(c)]
+        peers = [d for d in ranks if topo.rack(topo.host(d)) == topo.rack(topo.host(c))]
+        far = [d for d in ranks if d not in peers and topo.chip(d) == topo.chip(c) and topo.may_write(c, d)][0]
+        owners = [d for d in chip if d not in ranks and all(topo.may_write(d, e) for e in peers)]
+        near = [d for d in owners if topo.die(d) == topo.die(c)]
+        away = [d for d in owners if topo.die(d) != topo.die(c)]
+        info[c] = {"peers": peers, "far": far, "F": [near[0], away[0]], "Fs": near[1], "k": peers.index(c)}
+        role[c] = ("rank", c, 0)
+        role[near[0]] = ("fold", c, 0)
+        role[away[0]] = ("fold", c, 1)
+        role[near[1]] = ("sfold", c, 0)
+    return info, role
+
+
+def _engines(topo, src, off_dsts, on_dst):
+    m = topo.mask(src, off_dsts[0])
+    for d in off_dsts:
+        m &= topo.mask(src, d)
+    off = _bits(m)
+    on = [b for b in _bits(topo.mask(src, on_dst)) if b not in off]
+    return off, on
+
+
+def _dst(topo, d, src):
+    rid, pid = topo.addr(d, src)
+    return DstId(rid=rid, pnc=pid)
+
+
+def _folder(g, core, T, topo, info, c, srcs, land, sem, feed_sem, feed_n):
+    S = T.sem
+    outs = [d for d in info[c]["peers"] if d != c]
+    off, on = _engines(topo, core, outs, c)
+    g.wait_ge(feed_sem, feed_n)
+    g.remote_dma_fused([
+        RemoteDMATransfer(dst_ids=[_dst(topo, d, core) for d in outs], dma_engine_mask=_mk(off), remote_sem=sem,
+                          srcs=srcs, dsts=[land for d in outs], alu_op=1),
+        RemoteDMATransfer(dst_ids=[_dst(topo, c, core)], dma_engine_mask=_mk(on), remote_sem=sem,
+                          srcs=srcs, dsts=[land], alu_op=1),
+    ], local_sem=S.lsem)
+    g.wait_ge(S.lsem, len(off) + len(on))
+
+
+def rank_program(g, core, T, topo):
+    info, role = _plan(T, topo)
+    if core not in role:
+        return
+    kind, c, j = role[core]
+    S = T.sem
+    me = info[c]
+    far = info[me["far"]]
+    k = me["k"]
+    off, on = _engines(topo, c, far["F"] + [far["Fs"]], me["F"][0])
+    ho, hn = len(off) // 2, len(on) // 2
+
+    if kind == "fold":
+        _folder(g, core, T, topo, info, c, [T.fa[:], T.fb[:]], T["land%d" % j][:, k * H:(k + 1) * H],
+                S["arr%d_%d" % (k, j)], S.feed, ho + hn)
+        return
+    if kind == "sfold":
+        _folder(g, core, T, topo, info, c, [T.sfa[:], T.sfb[:]], T.sland[:, 2 * k:2 * k + 2],
+                S.sarr, S.sfeed, len(off) + len(on))
+        return
+
+    v, pe, act, sy = g.vector, g.tensor, g.scalar, g.sync
+    add, mult = AluOpType.add, AluOpType.mult
+
+    sy.dma_start(T.xs[:], T.x[:]).then_inc(S.ldx, 16)
+    act.dma_start(T.ws[:], T.w[:]).then_inc(S.ldw, 16)
+    v.memset(T.ones[:], 1.0).then_inc(S.c1, 1)
+    g.wait_ge(S.c1, 1)
+    g.affine_select(T.ident[:], T.ones[:], [[-1, H]], AluOpType.is_equal, 0.0, 0, 1).then_inc(S.cid, 1)
+
+    act.wait_ge(S.ldx, 16)
+    act.activation(T.sq[:], T.xs[:], ActivationFunctionType.Square).then_inc(S.sqd, 1)
+    pe.wait_ge(S.ldx, 16)
+    pe.wait_ge(S.ldw, 16)
+    pe.matmul(T.pp0[:, 0:H], T.ws[:], T.xs[:, 0:H], True, True).then_inc(S.mm0, 1)
+    pe.wait_ge(S.sqd, 1)
+    pe.wait_ge(S.c1, 1)
+    pe.matmul(T.ps[:, 0:1], T.sq[:, 0:H], T.ones[:, 0:1], True, True).then_inc(S.mms, 1)
+    pe.matmul(T.ps[:, 1:2], T.sq[:, H:2 * H], T.ones[:, 0:1], True, True).then_inc(S.mms, 1)
+    pe.matmul(T.pp1[:, 0:H], T.ws[:], T.xs[:, H:2 * H], True, True).then_inc(S.mm1, 1)
+    v.wait_ge(S.mm0, 1)
+    v.tensor_copy(T.pbuf[:, 0:H], T.pp0[:, 0:H]).then_inc(S.cp, 1)
+    v.wait_ge(S.mms, 2)
+    v.tensor_copy(T.sown[:], T.ps[:, 0:2]).then_inc(S.cps, 1)
+    v.wait_ge(S.mm1, 1)
+    v.tensor_copy(T.pbuf[:, H:2 * H], T.pp1[:, 0:H]).then_inc(S.cp, 1)
+
+    g.wait_ge(S.cps, 1)
+    g.remote_dma_fused([
+        RemoteDMATransfer(dst_ids=[_dst(topo, far["Fs"], core)], dma_engine_mask=_mk(off), remote_sem=S.sfeed,
+                          src=T.sown[:], dst=T.sfb[:]),
+        RemoteDMATransfer(dst_ids=[_dst(topo, me["Fs"], core)], dma_engine_mask=_mk(on), remote_sem=S.sfeed,
+                          src=T.sown[:], dst=T.sfa[:]),
+    ], local_sem=S.lsem)
+    g.wait_ge(S.cp, 2)
+    tr = []
+    for h in range(2):
+        half = T.pbuf[:, h * H:(h + 1) * H]
+        tr.append(RemoteDMATransfer(dst_ids=[_dst(topo, far["F"][h], core)], dma_engine_mask=_mk(off[h * ho:(h + 1) * ho]),
+                                    remote_sem=S.feed, src=half, dst=T.fb[:]))
+        tr.append(RemoteDMATransfer(dst_ids=[_dst(topo, me["F"][h], core)], dma_engine_mask=_mk(on[h * hn:(h + 1) * hn]),
+                                    remote_sem=S.feed, src=half, dst=T.fa[:]))
+    g.remote_dma_fused(tr, local_sem=S.lsem)
+
+    others = [d for d in me["peers"] if d != c]
+    others.sort(key=lambda d: (not topo.same_plane(c, d), topo.host(d) != topo.host(c)))
+    cnt = {}
+    for d in me["peers"]:
+        f = info[d]["F"][0]
+        foff, fon = _engines(topo, f, [e for e in me["peers"] if e != d], d)
+        cnt[info[d]["k"]] = len(fon) if d == c else len(foff)
+    ks = [k] + [info[d]["k"] for d in others]
+
+    v.wait_ge(S.sarr, sum(cnt.values()))
+    v.tensor_tensor(T.s4[:], T.sland[:, 0:4], T.sland[:, 4:8], add).then_inc(S.v1, 1)
+    v.wait_ge(S.v1, 1)
+    v.tensor_tensor(T.s2[:], T.s4[:, 0:2], T.s4[:, 2:4], add).then_inc(S.v2, 1)
+    act.wait_ge(S.v2, 1)
+    act.activation(T.rt[:], T.s2[:], ActivationFunctionType.Sqrt, bias=EPS, scale=1.0 / D).then_inc(S.a1, 1)
+    v.wait_ge(S.a1, 1)
+    v.reciprocal(T.rs[:], T.rt[:]).then_inc(S.v3, 1)
+    v.wait_ge(S.v3, 1)
+    v.wait_ge(S.cid, 1)
+    for h in range(2):
+        v.tensor_scalar(T.diag[:, h * H:(h + 1) * H], T.ident[:], T.rs[:, h:h + 1], None, mult).then_inc(S.v4, 1)
+    pe.wait_ge(S.v4, 2)
+    pe.matmul(T.pb0[:, 0:H], T.ones[:], T.diag[:, 0:H], True, True).then_inc(S.b0, 1)
+    pe.matmul(T.pb1[:, 0:H], T.ones[:], T.diag[:, H:2 * H], True, True).then_inc(S.b1, 1)
+
+    def slot(h, i):
+        return T["land%d" % h][:, ks[i] * H:(ks[i] + 1) * H]
+
+    def arrived(h, i):
+        v.wait_ge(S["arr%d_%d" % (ks[i], h)], cnt[ks[i]])
+
+    pa = [T.pa0[:, 0:H], T.pa1[:, 0:H]]
+    pb = [T.pb0[:, 0:H], T.pb1[:, 0:H]]
+    acc = [S.acc0, S.acc1]
+    for h in range(2):
+        arrived(h, 0)
+        arrived(h, 1)
+        v.tensor_tensor(pa[h], slot(h, 0), slot(h, 1), add).then_inc(acc[h], 1)
+    for h in range(2):
+        arrived(h, 2)
+        v.wait_ge(acc[h], 1)
+        v.tensor_tensor(pa[h], pa[h], slot(h, 2), add).then_inc(acc[h], 1)
+    for h in range(2):
+        cols = slice(h * H, (h + 1) * H)
+        arrived(h, 3)
+        v.wait_ge(acc[h], 2)
+        v.tensor_tensor(T.tb[:, cols], pa[h], slot(h, 3), add).then_inc(acc[h], 1)
+        v.wait_ge(acc[h], 3)
+        v.wait_ge([S.b0, S.b1][h], 1)
+        v.tensor_tensor(T.yb[:, cols], T.tb[:, cols], pb[h], mult).then_inc([S.yd0, S.yd1][h], 1)
+    sy.wait_ge(S.yd0, 1)
+    sy.dma_start(T.y[:, 0:H], T.yb[:, 0:H]).then_inc(S.st0, 16)
+    act.wait_ge(S.yd1, 1)
+    act.dma_start(T.y[:, H:2 * H], T.yb[:, H:2 * H]).then_inc(S.st1, 16)
+    g.wait_ge(S.lsem, 2 * (len(off) + len(on)))
+    sy.wait_ge(S.st0, 16)
+    act.wait_ge(S.st1, 16)

@@ -16,15 +16,17 @@ SCRATCH = {
     "sown": ("sbuf", [128, 2], "float32"),
     "fa": ("sbuf", [128, H], "float32"),
     "fb": ("sbuf", [128, H], "float32"),
-    "sfa": ("sbuf", [128, 2], "float32"),
-    "sfb": ("sbuf", [128, 2], "float32"),
+    "sda": ("dram", [128, 2], "float32"),
+    "sdb": ("dram", [128, 2], "float32"),
+    "sl": ("dram", [4, 128, 2], "float32"),
     "sland": ("sbuf", [128, 8], "float32"),
     "land0": ("sbuf", [128, 4 * H], "float32"),
     "land1": ("sbuf", [128, 4 * H], "float32"),
     "s4": ("sbuf", [128, 4], "float32"),
     "s2": ("sbuf", [128, 2], "float32"),
+    "vv": ("sbuf", [128, 2], "float32"),
     "rt": ("sbuf", [128, 2], "float32"),
-    "rs": ("sbuf", [128, 2], "float32"),
+    "rv": ("sbuf", [128, 2], "float32"),
     "diag": ("sbuf", [128, 2 * H], "float32"),
     "tb": ("sbuf", [128, 2 * H], "float32"),
     "yb": ("sbuf", [128, 2 * H], "float32"),
@@ -36,8 +38,9 @@ SCRATCH = {
     "pa0": ("psum", [128, 512], "float32"),
     "pa1": ("psum", [128, 512], "float32"),
 }
-SEMAPHORES = (["ldx", "ldw", "c1", "cid", "sqd", "mm0", "mms", "mm1", "cp", "cps", "lsem", "feed", "sfeed", "sarr",
-               "v1", "v2", "a1", "v3", "v4", "b0", "b1", "acc0", "acc1", "yd0", "yd1", "st0", "st1"]
+SEMAPHORES = (["ldx", "ldw", "c1", "cid", "sq0", "sq1", "mm0", "mms", "mm1", "cp0", "cp1", "cps", "lsem", "feed", "sfeed",
+               "sld", "v1", "v2", "v2b", "a1", "v3", "v4", "b0", "b1", "acc0", "acc1", "yd0", "yd1", "st0", "st1"]
+              + ["sarr%d" % k for k in range(4)]
               + ["arr%d_%d" % (k, j) for k in range(4) for j in range(2)])
 
 
@@ -61,11 +64,10 @@ def _plan(T, topo):
         owners = [d for d in chip if d not in ranks and all(topo.may_write(d, e) for e in peers)]
         near = [d for d in owners if topo.die(d) == topo.die(c)]
         away = [d for d in owners if topo.die(d) != topo.die(c)]
-        info[c] = {"peers": peers, "far": far, "F": [near[0], away[0]], "Fs": near[1], "k": peers.index(c)}
+        info[c] = {"peers": peers, "far": far, "F": [near[0], away[0]], "k": peers.index(c)}
         role[c] = ("rank", c, 0)
         role[near[0]] = ("fold", c, 0)
         role[away[0]] = ("fold", c, 1)
-        role[near[1]] = ("sfold", c, 0)
     return info, role
 
 
@@ -83,18 +85,16 @@ def _dst(topo, d, src):
     return DstId(rid=rid, pnc=pid)
 
 
-def _folder(g, core, T, topo, info, c, srcs, land, sem, feed_sem, feed_n):
-    S = T.sem
+def _fold(g, core, T, topo, info, c, srcs, land, sem):
     outs = [d for d in info[c]["peers"] if d != c]
     off, on = _engines(topo, core, outs, c)
-    g.wait_ge(feed_sem, feed_n)
     g.remote_dma_fused([
         RemoteDMATransfer(dst_ids=[_dst(topo, d, core) for d in outs], dma_engine_mask=_mk(off), remote_sem=sem,
                           srcs=srcs, dsts=[land for d in outs], alu_op=1),
         RemoteDMATransfer(dst_ids=[_dst(topo, c, core)], dma_engine_mask=_mk(on), remote_sem=sem,
                           srcs=srcs, dsts=[land], alu_op=1),
-    ], local_sem=S.lsem)
-    g.wait_ge(S.lsem, len(off) + len(on))
+    ], local_sem=T.sem.lsem)
+    return len(off) + len(on)
 
 
 def rank_program(g, core, T, topo):
@@ -106,16 +106,18 @@ def rank_program(g, core, T, topo):
     me = info[c]
     far = info[me["far"]]
     k = me["k"]
-    off, on = _engines(topo, c, far["F"] + [far["Fs"]], me["F"][0])
-    ho, hn = len(off) // 2, len(on) // 2
+    off, on = _engines(topo, c, far["F"], me["F"][0])
+    fed = len(off) + len(on)
 
     if kind == "fold":
-        _folder(g, core, T, topo, info, c, [T.fa[:], T.fb[:]], T["land%d" % j][:, k * H:(k + 1) * H],
-                S["arr%d_%d" % (k, j)], S.feed, ho + hn)
-        return
-    if kind == "sfold":
-        _folder(g, core, T, topo, info, c, [T.sfa[:], T.sfb[:]], T.sland[:, 2 * k:2 * k + 2],
-                S.sarr, S.sfeed, len(off) + len(on))
+        left = 0
+        if j == 1:
+            g.wait_ge(S.sfeed, fed)
+            left += _fold(g, core, T, topo, info, c, [T.sda[:], T.sdb[:]], T.sl[k], S["sarr%d" % k])
+        g.wait_ge(S.feed, fed)
+        left += _fold(g, core, T, topo, info, c, [T.fa[:], T.fb[:]], T["land%d" % j][:, k * H:(k + 1) * H],
+                      S["arr%d_%d" % (k, j)])
+        g.wait_ge(S.lsem, left)
         return
 
     v, pe, act, sy = g.vector, g.tensor, g.scalar, g.sync
@@ -128,38 +130,38 @@ def rank_program(g, core, T, topo):
     g.affine_select(T.ident[:], T.ones[:], [[-1, H]], AluOpType.is_equal, 0.0, 0, 1).then_inc(S.cid, 1)
 
     act.wait_ge(S.ldx, 16)
-    act.activation(T.sq[:], T.xs[:], ActivationFunctionType.Square).then_inc(S.sqd, 1)
+    act.activation(T.sq[:, 0:H], T.xs[:, 0:H], ActivationFunctionType.Square).then_inc(S.sq0, 1)
+    act.activation(T.sq[:, H:2 * H], T.xs[:, H:2 * H], ActivationFunctionType.Square).then_inc(S.sq1, 1)
+    pe.wait_ge(S.c1, 1)
+    pe.wait_ge(S.sq0, 1)
+    pe.matmul(T.ps[:, 0:1], T.sq[:, 0:H], T.ones[:, 0:1], True, True).then_inc(S.mms, 1)
+    pe.wait_ge(S.sq1, 1)
+    pe.matmul(T.ps[:, 1:2], T.sq[:, H:2 * H], T.ones[:, 0:1], True, True).then_inc(S.mms, 1)
     pe.wait_ge(S.ldx, 16)
     pe.wait_ge(S.ldw, 16)
     pe.matmul(T.pp0[:, 0:H], T.ws[:], T.xs[:, 0:H], True, True).then_inc(S.mm0, 1)
-    pe.wait_ge(S.sqd, 1)
-    pe.wait_ge(S.c1, 1)
-    pe.matmul(T.ps[:, 0:1], T.sq[:, 0:H], T.ones[:, 0:1], True, True).then_inc(S.mms, 1)
-    pe.matmul(T.ps[:, 1:2], T.sq[:, H:2 * H], T.ones[:, 0:1], True, True).then_inc(S.mms, 1)
     pe.matmul(T.pp1[:, 0:H], T.ws[:], T.xs[:, H:2 * H], True, True).then_inc(S.mm1, 1)
-    v.wait_ge(S.mm0, 1)
-    v.tensor_copy(T.pbuf[:, 0:H], T.pp0[:, 0:H]).then_inc(S.cp, 1)
     v.wait_ge(S.mms, 2)
     v.tensor_copy(T.sown[:], T.ps[:, 0:2]).then_inc(S.cps, 1)
+    v.wait_ge(S.mm0, 1)
+    v.tensor_copy(T.pbuf[:, 0:H], T.pp0[:, 0:H]).then_inc(S.cp0, 1)
     v.wait_ge(S.mm1, 1)
-    v.tensor_copy(T.pbuf[:, H:2 * H], T.pp1[:, 0:H]).then_inc(S.cp, 1)
+    v.tensor_copy(T.pbuf[:, H:2 * H], T.pp1[:, 0:H]).then_inc(S.cp1, 1)
+
+    def send(src, h, dst_far, dst_own, sem):
+        g.remote_dma_fused([
+            RemoteDMATransfer(dst_ids=[_dst(topo, far["F"][h], core)], dma_engine_mask=_mk(off), remote_sem=sem,
+                              src=src, dst=dst_far),
+            RemoteDMATransfer(dst_ids=[_dst(topo, me["F"][h], core)], dma_engine_mask=_mk(on), remote_sem=sem,
+                              src=src, dst=dst_own),
+        ], local_sem=S.lsem)
 
     g.wait_ge(S.cps, 1)
-    g.remote_dma_fused([
-        RemoteDMATransfer(dst_ids=[_dst(topo, far["Fs"], core)], dma_engine_mask=_mk(off), remote_sem=S.sfeed,
-                          src=T.sown[:], dst=T.sfb[:]),
-        RemoteDMATransfer(dst_ids=[_dst(topo, me["Fs"], core)], dma_engine_mask=_mk(on), remote_sem=S.sfeed,
-                          src=T.sown[:], dst=T.sfa[:]),
-    ], local_sem=S.lsem)
-    g.wait_ge(S.cp, 2)
-    tr = []
-    for h in range(2):
-        half = T.pbuf[:, h * H:(h + 1) * H]
-        tr.append(RemoteDMATransfer(dst_ids=[_dst(topo, far["F"][h], core)], dma_engine_mask=_mk(off[h * ho:(h + 1) * ho]),
-                                    remote_sem=S.feed, src=half, dst=T.fb[:]))
-        tr.append(RemoteDMATransfer(dst_ids=[_dst(topo, me["F"][h], core)], dma_engine_mask=_mk(on[h * hn:(h + 1) * hn]),
-                                    remote_sem=S.feed, src=half, dst=T.fa[:]))
-    g.remote_dma_fused(tr, local_sem=S.lsem)
+    send(T.sown[:], 1, T.sdb[:], T.sda[:], S.sfeed)
+    g.wait_ge(S.cp0, 1)
+    send(T.pbuf[:, 0:H], 0, T.fb[:], T.fa[:], S.feed)
+    g.wait_ge(S.cp1, 1)
+    send(T.pbuf[:, H:2 * H], 1, T.fb[:], T.fa[:], S.feed)
 
     others = [d for d in me["peers"] if d != c]
     others.sort(key=lambda d: (not topo.same_plane(c, d), topo.host(d) != topo.host(c)))
@@ -170,18 +172,27 @@ def rank_program(g, core, T, topo):
         cnt[info[d]["k"]] = len(fon) if d == c else len(foff)
     ks = [k] + [info[d]["k"] for d in others]
 
-    v.wait_ge(S.sarr, sum(cnt.values()))
+    for i, kk in enumerate(ks):
+        q = [sy, act][i % 2]
+        q.wait_ge(S["sarr%d" % kk], cnt[kk])
+        q.dma_start(T.sland[:, 2 * kk:2 * kk + 2], T.sl[kk]).then_inc(S.sld, 16)
+
+    v.wait_ge(S.sld, 16 * len(ks))
     v.tensor_tensor(T.s4[:], T.sland[:, 0:4], T.sland[:, 4:8], add).then_inc(S.v1, 1)
     v.wait_ge(S.v1, 1)
     v.tensor_tensor(T.s2[:], T.s4[:, 0:2], T.s4[:, 2:4], add).then_inc(S.v2, 1)
     act.wait_ge(S.v2, 1)
     act.activation(T.rt[:], T.s2[:], ActivationFunctionType.Sqrt, bias=EPS, scale=1.0 / D).then_inc(S.a1, 1)
-    v.wait_ge(S.a1, 1)
-    v.reciprocal(T.rs[:], T.rt[:]).then_inc(S.v3, 1)
+    v.wait_ge(S.v2, 1)
+    v.tensor_scalar(T.vv[:], T.s2[:], 1.0 / D, EPS, mult, add).then_inc(S.v2b, 1)
+    v.wait_ge(S.v2b, 1)
+    v.reciprocal(T.rv[:], T.vv[:]).then_inc(S.v3, 1)
     v.wait_ge(S.v3, 1)
+    v.wait_ge(S.a1, 1)
     v.wait_ge(S.cid, 1)
     for h in range(2):
-        v.tensor_scalar(T.diag[:, h * H:(h + 1) * H], T.ident[:], T.rs[:, h:h + 1], None, mult).then_inc(S.v4, 1)
+        v.tensor_scalar(T.diag[:, h * H:(h + 1) * H], T.ident[:], T.rt[:, h:h + 1], T.rv[:, h:h + 1],
+                        mult, mult).then_inc(S.v4, 1)
     pe.wait_ge(S.v4, 2)
     pe.matmul(T.pb0[:, 0:H], T.ones[:], T.diag[:, 0:H], True, True).then_inc(S.b0, 1)
     pe.matmul(T.pb1[:, 0:H], T.ones[:], T.diag[:, H:2 * H], True, True).then_inc(S.b1, 1)
@@ -215,6 +226,6 @@ def rank_program(g, core, T, topo):
     sy.dma_start(T.y[:, 0:H], T.yb[:, 0:H]).then_inc(S.st0, 16)
     act.wait_ge(S.yd1, 1)
     act.dma_start(T.y[:, H:2 * H], T.yb[:, H:2 * H]).then_inc(S.st1, 16)
-    g.wait_ge(S.lsem, 2 * (len(off) + len(on)))
+    g.wait_ge(S.lsem, 3 * fed)
     sy.wait_ge(S.st0, 16)
     act.wait_ge(S.st1, 16)

@@ -3,45 +3,51 @@ from concourse.mybir import AluOpType, ActivationFunctionType
 
 N = 8
 H = 128
+TK = 256
+A = 136
+B = 60
+W = [A, 2 * B]
+O = [0, A]
+FW = [A, B, B]
 D = 128 * N
 EPS = 0.01
 
 SCRATCH = {
-    "xs": ("sbuf", [128, 2 * H], "float32"),
+    "xs": ("sbuf", [128, TK], "float32"),
     "ws": ("sbuf", [128, H], "float32"),
-    "sq": ("sbuf", [128, 2 * H], "float32"),
+    "sq": ("sbuf", [128, TK], "float32"),
     "ones": ("sbuf", [128, H], "float32"),
     "ident": ("sbuf", [128, H], "float32"),
-    "pbuf": ("sbuf", [128, 2 * H], "float32"),
+    "pbuf": ("sbuf", [128, TK], "float32"),
     "sown": ("sbuf", [128, 2], "float32"),
-    "fa": ("sbuf", [128, H], "float32"),
-    "fb": ("sbuf", [128, H], "float32"),
+    "fa": ("sbuf", [128, A], "float32"),
+    "fb": ("sbuf", [128, A], "float32"),
     "sda": ("dram", [128, 2], "float32"),
     "sdb": ("dram", [128, 2], "float32"),
-    "sl": ("dram", [4, 128, 2], "float32"),
-    "sland": ("sbuf", [128, 8], "float32"),
-    "land0": ("sbuf", [128, 4 * H], "float32"),
-    "land1": ("sbuf", [128, 4 * H], "float32"),
+    "sl": ("dram", [N, 128, 2], "float32"),
+    "sland": ("sbuf", [128, 2 * N], "float32"),
+    "land0": ("sbuf", [128, 4 * W[0]], "float32"),
+    "land1": ("sbuf", [128, 4 * W[1]], "float32"),
+    "s8": ("sbuf", [128, 8], "float32"),
     "s4": ("sbuf", [128, 4], "float32"),
     "s2": ("sbuf", [128, 2], "float32"),
     "vv": ("sbuf", [128, 2], "float32"),
     "rt": ("sbuf", [128, 2], "float32"),
     "rv": ("sbuf", [128, 2], "float32"),
-    "diag": ("sbuf", [128, 2 * H], "float32"),
-    "tb": ("sbuf", [128, 2 * H], "float32"),
-    "yb": ("sbuf", [128, 2 * H], "float32"),
+    "diag": ("sbuf", [128, TK], "float32"),
+    "tb": ("sbuf", [128, TK], "float32"),
+    "yb": ("sbuf", [128, TK], "float32"),
     "pp0": ("psum", [128, 512], "float32"),
     "pp1": ("psum", [128, 512], "float32"),
     "ps": ("psum", [128, 512], "float32"),
-    "pb0": ("psum", [128, 512], "float32"),
-    "pb1": ("psum", [128, 512], "float32"),
+    "pb": ("psum", [128, 512], "float32"),
     "pa0": ("psum", [128, 512], "float32"),
     "pa1": ("psum", [128, 512], "float32"),
 }
 SEMAPHORES = (["ldx", "ldw", "c1", "cid", "sq0", "sq1", "mm0", "mms", "mm1", "cp0", "cp1", "cps", "lsem", "feed", "sfeed",
-               "sld", "v1", "v2", "v2b", "a1", "v3", "v4", "b0", "b1", "acc0", "acc1", "yd0", "yd1", "st0", "st1"]
-              + ["sarr%d" % k for k in range(4)]
-              + ["arr%d_%d" % (k, j) for k in range(4) for j in range(2)])
+               "sld", "v0", "v1", "v2", "v2b", "a1", "v3", "v4", "bb", "acc0", "acc1", "yd0", "yd1", "st0", "st1"]
+              + ["sarr%d" % r for r in range(N)]
+              + ["arr%d_%d" % (k, j) for k in range(4) for j in range(3)])
 
 
 def _bits(m):
@@ -64,10 +70,10 @@ def _plan(T, topo):
         owners = [d for d in chip if d not in ranks and all(topo.may_write(d, e) for e in peers)]
         near = [d for d in owners if topo.die(d) == topo.die(c)]
         away = [d for d in owners if topo.die(d) != topo.die(c)]
-        info[c] = {"peers": peers, "far": far, "F": [near[0], away[0]], "k": peers.index(c)}
+        info[c] = {"peers": peers, "far": far, "F": [away[0], near[0], near[1]], "k": peers.index(c)}
         role[c] = ("rank", c, 0)
-        role[near[0]] = ("fold", c, 0)
-        role[away[0]] = ("fold", c, 1)
+        for j, f in enumerate(info[c]["F"]):
+            role[f] = ("fold", c, j)
     return info, role
 
 
@@ -80,21 +86,26 @@ def _engines(topo, src, off_dsts, on_dst):
     return off, on
 
 
+def _fold_engines(topo, info, f, c):
+    off, on = _engines(topo, f, [d for d in info[c]["peers"] if d != c], c)
+    return off, on[::2]
+
+
 def _dst(topo, d, src):
     rid, pid = topo.addr(d, src)
     return DstId(rid=rid, pnc=pid)
 
 
-def _fold(g, core, T, topo, info, c, srcs, land, sem):
-    outs = [d for d in info[c]["peers"] if d != c]
-    off, on = _engines(topo, core, outs, c)
-    g.remote_dma_fused([
-        RemoteDMATransfer(dst_ids=[_dst(topo, d, core) for d in outs], dma_engine_mask=_mk(off), remote_sem=sem,
-                          srcs=srcs, dsts=[land for d in outs], alu_op=1),
-        RemoteDMATransfer(dst_ids=[_dst(topo, c, core)], dma_engine_mask=_mk(on), remote_sem=sem,
-                          srcs=srcs, dsts=[land], alu_op=1),
-    ], local_sem=T.sem.lsem)
-    return len(off) + len(on)
+def _spread(g, core, T, topo, info, c, srcs, land, sem, outs, own):
+    off, on = _fold_engines(topo, info, core, c)
+    op = 1 if len(srcs) > 1 else 0
+    tr = [RemoteDMATransfer(dst_ids=[_dst(topo, d, core) for d in outs], dma_engine_mask=_mk(off), remote_sem=sem,
+                            srcs=srcs, dsts=[land for d in outs], alu_op=op)]
+    if own:
+        tr.append(RemoteDMATransfer(dst_ids=[_dst(topo, c, core)], dma_engine_mask=_mk(on), remote_sem=sem,
+                                    srcs=srcs, dsts=[land], alu_op=op))
+    g.remote_dma_fused(tr, local_sem=T.sem.lsem)
+    return len(off) + (len(on) if own else 0)
 
 
 def rank_program(g, core, T, topo):
@@ -110,18 +121,29 @@ def rank_program(g, core, T, topo):
     fed = len(off) + len(on)
 
     if kind == "fold":
-        left = 0
-        if j == 1:
-            g.wait_ge(S.sfeed, fed)
-            left += _fold(g, core, T, topo, info, c, [T.sda[:], T.sdb[:]], T.sl[k], S["sarr%d" % k])
-        g.wait_ge(S.feed, fed)
-        left += _fold(g, core, T, topo, info, c, [T.fa[:], T.fb[:]], T["land%d" % j][:, k * H:(k + 1) * H],
-                      S["arr%d_%d" % (k, j)])
+        rest = [d for d in me["peers"] if d != c]
+        if j == 0:
+            r = T.rank_of(me["far"])
+            g.wait_ge(S.sfeed, len(off))
+            left = _spread(g, core, T, topo, info, c, [T.sdb[:]], T.sl[r], S["sarr%d" % r], rest, True)
+            g.wait_ge(S.feed, fed)
+            land = T.land0[:, k * A:(k + 1) * A]
+        else:
+            r = T.rank_of(c)
+            outs = [d for d in rest if topo.same_plane(c, d) == (j == 2)]
+            g.wait_ge(S.sfeed, len(on) // 2)
+            left = _spread(g, core, T, topo, info, c, [T.sda[:]], T.sl[r], S["sarr%d" % r], outs, False)
+            g.wait_ge(S.feed, fed // 2)
+            land = T.land1[:, k * 2 * B + (j - 1) * B:k * 2 * B + j * B]
+        left += _spread(g, core, T, topo, info, c, [T.fa[:, 0:FW[j]], T.fb[:, 0:FW[j]]], land,
+                        S["arr%d_%d" % (k, j)], rest, True)
         g.wait_ge(S.lsem, left)
         return
 
     v, pe, act, sy = g.vector, g.tensor, g.scalar, g.sync
     add, mult = AluOpType.add, AluOpType.mult
+    cols = [slice(O[h], O[h] + W[h]) for h in range(2)]
+    mine = T.rank_of(c)
 
     sy.dma_start(T.xs[:], T.x[:]).then_inc(S.ldx, 16)
     act.dma_start(T.ws[:], T.w[:]).then_inc(S.ldw, 16)
@@ -139,46 +161,55 @@ def rank_program(g, core, T, topo):
     pe.matmul(T.ps[:, 1:2], T.sq[:, H:2 * H], T.ones[:, 0:1], True, True).then_inc(S.mms, 1)
     pe.wait_ge(S.ldx, 16)
     pe.wait_ge(S.ldw, 16)
-    pe.matmul(T.pp0[:, 0:H], T.ws[:], T.xs[:, 0:H], True, True).then_inc(S.mm0, 1)
-    pe.matmul(T.pp1[:, 0:H], T.ws[:], T.xs[:, H:2 * H], True, True).then_inc(S.mm1, 1)
+    pe.matmul(T.pp0[:, 0:W[0]], T.ws[:], T.xs[:, cols[0]], True, True).then_inc(S.mm0, 1)
+    pe.matmul(T.pp1[:, 0:W[1]], T.ws[:], T.xs[:, cols[1]], True, True).then_inc(S.mm1, 1)
     v.wait_ge(S.mms, 2)
     v.tensor_copy(T.sown[:], T.ps[:, 0:2]).then_inc(S.cps, 1)
     v.wait_ge(S.mm0, 1)
-    v.tensor_copy(T.pbuf[:, 0:H], T.pp0[:, 0:H]).then_inc(S.cp0, 1)
+    v.tensor_copy(T.pbuf[:, cols[0]], T.pp0[:, 0:W[0]]).then_inc(S.cp0, 1)
     v.wait_ge(S.mm1, 1)
-    v.tensor_copy(T.pbuf[:, H:2 * H], T.pp1[:, 0:H]).then_inc(S.cp1, 1)
+    v.tensor_copy(T.pbuf[:, cols[1]], T.pp1[:, 0:W[1]]).then_inc(S.cp1, 1)
 
-    def send(src, h, dst_far, dst_own, sem):
-        g.remote_dma_fused([
-            RemoteDMATransfer(dst_ids=[_dst(topo, far["F"][h], core)], dma_engine_mask=_mk(off), remote_sem=sem,
-                              src=src, dst=dst_far),
-            RemoteDMATransfer(dst_ids=[_dst(topo, me["F"][h], core)], dma_engine_mask=_mk(on), remote_sem=sem,
-                              src=src, dst=dst_own),
-        ], local_sem=S.lsem)
+    def tr(src, f, eng, dst, sem):
+        return RemoteDMATransfer(dst_ids=[_dst(topo, f, core)], dma_engine_mask=_mk(eng), remote_sem=sem, src=src, dst=dst)
 
+    ho, hn = len(off) // 2, len(on) // 2
+    offs, ons = [off[:ho], off[ho:]], [on[:hn], on[hn:]]
     g.wait_ge(S.cps, 1)
-    send(T.sown[:], 1, T.sdb[:], T.sda[:], S.sfeed)
+    g.remote_dma_fused([tr(T.sown[:], far["F"][0], off, T.sdb[:], S.sfeed)]
+                       + [tr(T.sown[:], me["F"][1 + i], ons[i], T.sda[:], S.sfeed) for i in range(2)], local_sem=S.lsem)
     g.wait_ge(S.cp0, 1)
-    send(T.pbuf[:, 0:H], 0, T.fb[:], T.fa[:], S.feed)
+    g.remote_dma_fused([tr(T.pbuf[:, cols[0]], far["F"][0], off, T.fb[:, 0:A], S.feed),
+                        tr(T.pbuf[:, cols[0]], me["F"][0], on, T.fa[:, 0:A], S.feed)], local_sem=S.lsem)
     g.wait_ge(S.cp1, 1)
-    send(T.pbuf[:, H:2 * H], 1, T.fb[:], T.fa[:], S.feed)
+    late = [T.pbuf[:, A + i * B:A + (i + 1) * B] for i in range(2)]
+    g.remote_dma_fused([tr(late[i], far["F"][1 + i], offs[i], T.fb[:, 0:B], S.feed) for i in range(2)]
+                       + [tr(late[i], me["F"][1 + i], ons[i], T.fa[:, 0:B], S.feed) for i in range(2)], local_sem=S.lsem)
 
     others = [d for d in me["peers"] if d != c]
     others.sort(key=lambda d: (not topo.same_plane(c, d), topo.host(d) != topo.host(c)))
     cnt = {}
     for d in me["peers"]:
-        f = info[d]["F"][0]
-        foff, fon = _engines(topo, f, [e for e in me["peers"] if e != d], d)
-        cnt[info[d]["k"]] = len(fon) if d == c else len(foff)
-    ks = [k] + [info[d]["k"] for d in others]
+        foff, fon = _fold_engines(topo, info, info[d]["F"][0], d)
+        cnt[d] = len(fon) if d == c else len(foff)
+    order = [c] + others
+    ks = [info[d]["k"] for d in order]
 
-    for i, kk in enumerate(ks):
-        q = [sy, act][i % 2]
-        q.wait_ge(S["sarr%d" % kk], cnt[kk])
-        q.dma_start(T.sland[:, 2 * kk:2 * kk + 2], T.sl[kk]).then_inc(S.sld, 16)
+    sy.wait_ge(S.cps, 1)
+    sy.dma_start(T.sland[:, 2 * mine:2 * mine + 2], T.sown[:]).then_inc(S.sld, 16)
+    got = [(T.rank_of(me["far"]), cnt[c])]
+    for d in others:
+        got.append((T.rank_of(d), cnt[d]))
+        got.append((T.rank_of(info[d]["far"]), cnt[d]))
+    for i, (r, n_inc) in enumerate(got):
+        q = [act, sy][i % 2]
+        q.wait_ge(S["sarr%d" % r], n_inc)
+        q.dma_start(T.sland[:, 2 * r:2 * r + 2], T.sl[r]).then_inc(S.sld, 16)
 
-    v.wait_ge(S.sld, 16 * len(ks))
-    v.tensor_tensor(T.s4[:], T.sland[:, 0:4], T.sland[:, 4:8], add).then_inc(S.v1, 1)
+    v.wait_ge(S.sld, 16 * (len(got) + 1))
+    v.tensor_tensor(T.s8[:], T.sland[:, 0:8], T.sland[:, 8:16], add).then_inc(S.v0, 1)
+    v.wait_ge(S.v0, 1)
+    v.tensor_tensor(T.s4[:], T.s8[:, 0:4], T.s8[:, 4:8], add).then_inc(S.v1, 1)
     v.wait_ge(S.v1, 1)
     v.tensor_tensor(T.s2[:], T.s4[:, 0:2], T.s4[:, 2:4], add).then_inc(S.v2, 1)
     act.wait_ge(S.v2, 1)
@@ -194,17 +225,17 @@ def rank_program(g, core, T, topo):
         v.tensor_scalar(T.diag[:, h * H:(h + 1) * H], T.ident[:], T.rt[:, h:h + 1], T.rv[:, h:h + 1],
                         mult, mult).then_inc(S.v4, 1)
     pe.wait_ge(S.v4, 2)
-    pe.matmul(T.pb0[:, 0:H], T.ones[:], T.diag[:, 0:H], True, True).then_inc(S.b0, 1)
-    pe.matmul(T.pb1[:, 0:H], T.ones[:], T.diag[:, H:2 * H], True, True).then_inc(S.b1, 1)
+    pe.matmul(T.pb[:, 0:H], T.ones[:], T.diag[:, 0:H], True, True).then_inc(S.bb, 1)
+    pe.matmul(T.pb[:, H:2 * H], T.ones[:], T.diag[:, H:2 * H], True, True).then_inc(S.bb, 1)
 
     def slot(h, i):
-        return T["land%d" % h][:, ks[i] * H:(ks[i] + 1) * H]
+        return T["land%d" % h][:, ks[i] * W[h]:(ks[i] + 1) * W[h]]
 
     def arrived(h, i):
-        v.wait_ge(S["arr%d_%d" % (ks[i], h)], cnt[ks[i]])
+        for jj in ([0], [1, 2])[h]:
+            v.wait_ge(S["arr%d_%d" % (ks[i], jj)], cnt[order[i]])
 
-    pa = [T.pa0[:, 0:H], T.pa1[:, 0:H]]
-    pb = [T.pb0[:, 0:H], T.pb1[:, 0:H]]
+    pa = [T.pa0[:, 0:W[0]], T.pa1[:, 0:W[1]]]
     acc = [S.acc0, S.acc1]
     for h in range(2):
         arrived(h, 0)
@@ -215,17 +246,16 @@ def rank_program(g, core, T, topo):
         v.wait_ge(acc[h], 1)
         v.tensor_tensor(pa[h], pa[h], slot(h, 2), add).then_inc(acc[h], 1)
     for h in range(2):
-        cols = slice(h * H, (h + 1) * H)
         arrived(h, 3)
         v.wait_ge(acc[h], 2)
-        v.tensor_tensor(T.tb[:, cols], pa[h], slot(h, 3), add).then_inc(acc[h], 1)
+        v.tensor_tensor(T.tb[:, cols[h]], pa[h], slot(h, 3), add).then_inc(acc[h], 1)
         v.wait_ge(acc[h], 3)
-        v.wait_ge([S.b0, S.b1][h], 1)
-        v.tensor_tensor(T.yb[:, cols], T.tb[:, cols], pb[h], mult).then_inc([S.yd0, S.yd1][h], 1)
+        v.wait_ge(S.bb, 2)
+        v.tensor_tensor(T.yb[:, cols[h]], T.tb[:, cols[h]], T.pb[:, cols[h]], mult).then_inc([S.yd0, S.yd1][h], 1)
     sy.wait_ge(S.yd0, 1)
-    sy.dma_start(T.y[:, 0:H], T.yb[:, 0:H]).then_inc(S.st0, 16)
+    sy.dma_start(T.y[:, cols[0]], T.yb[:, cols[0]]).then_inc(S.st0, 16)
     act.wait_ge(S.yd1, 1)
-    act.dma_start(T.y[:, H:2 * H], T.yb[:, H:2 * H]).then_inc(S.st1, 16)
+    act.dma_start(T.y[:, cols[1]], T.yb[:, cols[1]]).then_inc(S.st1, 16)
     g.wait_ge(S.lsem, 3 * fed)
     sy.wait_ge(S.st0, 16)
     act.wait_ge(S.st1, 16)

from concourse.bass import DstId, RemoteDMATransfer
from concourse.mybir import AluOpType, ActivationFunctionType

N = 8
H = 128
TK = 256
A = 136
B = 60
W = [A, 2 * B]
O = [0, A]
FW = [A, B, B]
D = 128 * N
EPS = 0.01

SCRATCH = {
    "xs": ("sbuf", [128, TK], "float32"),
    "ws": ("sbuf", [128, H], "float32"),
    "sq": ("sbuf", [128, TK], "float32"),
    "ones": ("sbuf", [128, H], "float32"),
    "ident": ("sbuf", [128, H], "float32"),
    "pbuf": ("sbuf", [128, TK], "float32"),
    "sown": ("sbuf", [128, 2], "float32"),
    "fa": ("sbuf", [128, A], "float32"),
    "fb": ("sbuf", [128, A], "float32"),
    "sda": ("dram", [128, 2], "float32"),
    "sdb": ("dram", [128, 2], "float32"),
    "sl": ("dram", [N, 128, 2], "float32"),
    "sland": ("sbuf", [128, 2 * N], "float32"),
    "land0": ("sbuf", [128, 4 * W[0]], "float32"),
    "land1": ("sbuf", [128, 4 * W[1]], "float32"),
    "s8": ("sbuf", [128, 8], "float32"),
    "s4": ("sbuf", [128, 4], "float32"),
    "s2": ("sbuf", [128, 2], "float32"),
    "vv": ("sbuf", [128, 2], "float32"),
    "rt": ("sbuf", [128, 2], "float32"),
    "rv": ("sbuf", [128, 2], "float32"),
    "diag": ("sbuf", [128, TK], "float32"),
    "tb": ("sbuf", [128, TK], "float32"),
    "yb": ("sbuf", [128, TK], "float32"),
    "pp0": ("psum", [128, 512], "float32"),
    "pp1": ("psum", [128, 512], "float32"),
    "ps": ("psum", [128, 512], "float32"),
    "pb": ("psum", [128, 512], "float32"),
    "pa0": ("psum", [128, 512], "float32"),
    "pa1": ("psum", [128, 512], "float32"),
}
SEMAPHORES = (["ldx", "ldw", "c1", "cid", "sq0", "sq1", "mm0", "mms", "mm1", "cp0", "cp1", "cps", "lsem", "feed", "sfeed",
               "sld", "v0", "v1", "v2", "v2b", "a1", "v3", "v4", "bb", "acc0", "acc1", "yd0", "yd1", "st0", "st1"]
              + ["sarr%d" % r for r in range(N)]
              + ["arr%d_%d" % (k, j) for k in range(4) for j in range(3)])


def _bits(m):
    return [i for i in range(m.bit_length()) if (m >> i) & 1]


def _mk(bits):
    return sum(1 << i for i in bits)


def _plan(T, topo):
    ranks = list(T.cores)
    info, role = {}, {}
    n = topo.CORES_PER_CHIP
    for c in ranks:
        chip = [d for d in range(max(0, c - n + 1), c + n)
                if topo.host(d) == topo.host(c) and topo.chip(d) == topo.chip(c)]
        peers = [d for d in ranks if topo.rack(topo.host(d)) == topo.rack(topo.host(c))]
        far = [d for d in ranks if d not in peers and topo.chip(d) == topo.chip(c) and topo.may_write(c, d)][0]
        owners = [d for d in chip if d not in ranks and all(topo.may_write(d, e) for e in peers)]
        near = [d for d in owners if topo.die(d) == topo.die(c)]
        away = [d for d in owners if topo.die(d) != topo.die(c)]
        info[c] = {"peers": peers, "far": far, "F": [away[0], near[0], near[1]], "k": peers.index(c)}
        role[c] = ("rank", c, 0)
        for j, f in enumerate(info[c]["F"]):
            role[f] = ("fold", c, j)
    return info, role


def _engines(topo, src, off_dsts, on_dst):
    m = topo.mask(src, off_dsts[0])
    for d in off_dsts:
        m &= topo.mask(src, d)
    off = _bits(m)
    on = [b for b in _bits(topo.mask(src, on_dst)) if b not in off]
    return off, on


def _fold_engines(topo, info, f, c):
    off, on = _engines(topo, f, [d for d in info[c]["peers"] if d != c], c)
    return off, on[::2]


def _dst(topo, d, src):
    rid, pid = topo.addr(d, src)
    return DstId(rid=rid, pnc=pid)


def _spread(g, core, T, topo, info, c, srcs, land, sem, outs, own):
    off, on = _fold_engines(topo, info, core, c)
    op = 1 if len(srcs) > 1 else 0
    tr = [RemoteDMATransfer(dst_ids=[_dst(topo, d, core) for d in outs], dma_engine_mask=_mk(off), remote_sem=sem,
                            srcs=srcs, dsts=[land for d in outs], alu_op=op)]
    if own:
        tr.append(RemoteDMATransfer(dst_ids=[_dst(topo, c, core)], dma_engine_mask=_mk(on), remote_sem=sem,
                                    srcs=srcs, dsts=[land], alu_op=op))
    g.remote_dma_fused(tr, local_sem=T.sem.lsem)
    return len(off) + (len(on) if own else 0)


def rank_program(g, core, T, topo):
    info, role = _plan(T, topo)
    if core not in role:
        return
    kind, c, j = role[core]
    S = T.sem
    me = info[c]
    far = info[me["far"]]
    k = me["k"]
    off, on = _engines(topo, c, far["F"], me["F"][0])
    fed = len(off) + len(on)

    if kind == "fold":
        rest = [d for d in me["peers"] if d != c]
        if j == 0:
            r = T.rank_of(me["far"])
            g.wait_ge(S.sfeed, len(off))
            left = _spread(g, core, T, topo, info, c, [T.sdb[:]], T.sl[r], S["sarr%d" % r], rest, True)
            g.wait_ge(S.feed, fed)
            land = T.land0[:, k * A:(k + 1) * A]
        else:
            r = T.rank_of(c)
            outs = [d for d in rest if topo.same_plane(c, d) == (j == 2)]
            g.wait_ge(S.sfeed, len(on) // 2)
            left = _spread(g, core, T, topo, info, c, [T.sda[:]], T.sl[r], S["sarr%d" % r], outs, False)
            g.wait_ge(S.feed, fed // 2)
            land = T.land1[:, k * 2 * B + (j - 1) * B:k * 2 * B + j * B]
        left += _spread(g, core, T, topo, info, c, [T.fa[:, 0:FW[j]], T.fb[:, 0:FW[j]]], land,
                        S["arr%d_%d" % (k, j)], rest, True)
        g.wait_ge(S.lsem, left)
        return

    v, pe, act, sy = g.vector, g.tensor, g.scalar, g.sync
    add, mult = AluOpType.add, AluOpType.mult
    cols = [slice(O[h], O[h] + W[h]) for h in range(2)]
    mine = T.rank_of(c)

    sy.dma_start(T.xs[:], T.x[:]).then_inc(S.ldx, 16)
    act.dma_start(T.ws[:], T.w[:]).then_inc(S.ldw, 16)
    v.memset(T.ones[:], 1.0).then_inc(S.c1, 1)
    g.wait_ge(S.c1, 1)
    g.affine_select(T.ident[:], T.ones[:], [[-1, H]], AluOpType.is_equal, 0.0, 0, 1).then_inc(S.cid, 1)

    act.wait_ge(S.ldx, 16)
    act.activation(T.sq[:, 0:H], T.xs[:, 0:H], ActivationFunctionType.Square).then_inc(S.sq0, 1)
    act.activation(T.sq[:, H:2 * H], T.xs[:, H:2 * H], ActivationFunctionType.Square).then_inc(S.sq1, 1)
    pe.wait_ge(S.c1, 1)
    pe.wait_ge(S.sq0, 1)
    pe.matmul(T.ps[:, 0:1], T.sq[:, 0:H], T.ones[:, 0:1], True, True).then_inc(S.mms, 1)
    pe.wait_ge(S.sq1, 1)
    pe.matmul(T.ps[:, 1:2], T.sq[:, H:2 * H], T.ones[:, 0:1], True, True).then_inc(S.mms, 1)
    pe.wait_ge(S.ldx, 16)
    pe.wait_ge(S.ldw, 16)
    pe.matmul(T.pp0[:, 0:W[0]], T.ws[:], T.xs[:, cols[0]], True, True).then_inc(S.mm0, 1)
    pe.matmul(T.pp1[:, 0:W[1]], T.ws[:], T.xs[:, cols[1]], True, True).then_inc(S.mm1, 1)
    v.wait_ge(S.mms, 2)
    v.tensor_copy(T.sown[:], T.ps[:, 0:2]).then_inc(S.cps, 1)
    v.wait_ge(S.mm0, 1)
    v.tensor_copy(T.pbuf[:, cols[0]], T.pp0[:, 0:W[0]]).then_inc(S.cp0, 1)
    v.wait_ge(S.mm1, 1)
    v.tensor_copy(T.pbuf[:, cols[1]], T.pp1[:, 0:W[1]]).then_inc(S.cp1, 1)

    def tr(src, f, eng, dst, sem):
        return RemoteDMATransfer(dst_ids=[_dst(topo, f, core)], dma_engine_mask=_mk(eng), remote_sem=sem, src=src, dst=dst)

    ho, hn = len(off) // 2, len(on) // 2
    offs, ons = [off[:ho], off[ho:]], [on[:hn], on[hn:]]
    g.wait_ge(S.cps, 1)
    g.remote_dma_fused([tr(T.sown[:], far["F"][0], off, T.sdb[:], S.sfeed)]
                       + [tr(T.sown[:], me["F"][1 + i], ons[i], T.sda[:], S.sfeed) for i in range(2)], local_sem=S.lsem)
    g.wait_ge(S.cp0, 1)
    g.remote_dma_fused([tr(T.pbuf[:, cols[0]], far["F"][0], off, T.fb[:, 0:A], S.feed),
                        tr(T.pbuf[:, cols[0]], me["F"][0], on, T.fa[:, 0:A], S.feed)], local_sem=S.lsem)
    g.wait_ge(S.cp1, 1)
    late = [T.pbuf[:, A + i * B:A + (i + 1) * B] for i in range(2)]
    g.remote_dma_fused([tr(late[i], far["F"][1 + i], offs[i], T.fb[:, 0:B], S.feed) for i in range(2)]
                       + [tr(late[i], me["F"][1 + i], ons[i], T.fa[:, 0:B], S.feed) for i in range(2)], local_sem=S.lsem)

    others = [d for d in me["peers"] if d != c]
    others.sort(key=lambda d: (not topo.same_plane(c, d), topo.host(d) != topo.host(c)))
    cnt = {}
    for d in me["peers"]:
        foff, fon = _fold_engines(topo, info, info[d]["F"][0], d)
        cnt[d] = len(fon) if d == c else len(foff)
    order = [c] + others
    ks = [info[d]["k"] for d in order]

    sy.wait_ge(S.cps, 1)
    sy.dma_start(T.sland[:, 2 * mine:2 * mine + 2], T.sown[:]).then_inc(S.sld, 16)
    got = [(T.rank_of(me["far"]), cnt[c])]
    for d in others:
        got.append((T.rank_of(d), cnt[d]))
        got.append((T.rank_of(info[d]["far"]), cnt[d]))
    for i, (r, n_inc) in enumerate(got):
        q = [act, sy][i % 2]
        q.wait_ge(S["sarr%d" % r], n_inc)
        q.dma_start(T.sland[:, 2 * r:2 * r + 2], T.sl[r]).then_inc(S.sld, 16)

    v.wait_ge(S.sld, 16 * (len(got) + 1))
    v.tensor_tensor(T.s8[:], T.sland[:, 0:8], T.sland[:, 8:16], add).then_inc(S.v0, 1)
    v.wait_ge(S.v0, 1)
    v.tensor_tensor(T.s4[:], T.s8[:, 0:4], T.s8[:, 4:8], add).then_inc(S.v1, 1)
    v.wait_ge(S.v1, 1)
    v.tensor_tensor(T.s2[:], T.s4[:, 0:2], T.s4[:, 2:4], add).then_inc(S.v2, 1)
    act.wait_ge(S.v2, 1)
    act.activation(T.rt[:], T.s2[:], ActivationFunctionType.Sqrt, bias=EPS, scale=1.0 / D).then_inc(S.a1, 1)
    v.wait_ge(S.v2, 1)
    v.tensor_scalar(T.vv[:], T.s2[:], 1.0 / D, EPS, mult, add).then_inc(S.v2b, 1)
    v.wait_ge(S.v2b, 1)
    v.reciprocal(T.rv[:], T.vv[:]).then_inc(S.v3, 1)
    v.wait_ge(S.v3, 1)
    v.wait_ge(S.a1, 1)
    v.wait_ge(S.cid, 1)
    for h in range(2):
        v.tensor_scalar(T.diag[:, h * H:(h + 1) * H], T.ident[:], T.rt[:, h:h + 1], T.rv[:, h:h + 1],
                        mult, mult).then_inc(S.v4, 1)
    pe.wait_ge(S.v4, 2)
    pe.matmul(T.pb[:, 0:H], T.ones[:], T.diag[:, 0:H], True, True).then_inc(S.bb, 1)
    pe.matmul(T.pb[:, H:2 * H], T.ones[:], T.diag[:, H:2 * H], True, True).then_inc(S.bb, 1)

    def slot(h, i):
        return T["land%d" % h][:, ks[i] * W[h]:(ks[i] + 1) * W[h]]

    def arrived(h, i):
        for jj in ([0], [1, 2])[h]:
            v.wait_ge(S["arr%d_%d" % (ks[i], jj)], cnt[order[i]])

    pa = [T.pa0[:, 0:W[0]], T.pa1[:, 0:W[1]]]
    acc = [S.acc0, S.acc1]
    for h in range(2):
        arrived(h, 0)
        arrived(h, 1)
        v.tensor_tensor(pa[h], slot(h, 0), slot(h, 1), add).then_inc(acc[h], 1)
    for h in range(2):
        arrived(h, 2)
        v.wait_ge(acc[h], 1)
        v.tensor_tensor(pa[h], pa[h], slot(h, 2), add).then_inc(acc[h], 1)
    for h in range(2):
        arrived(h, 3)
        v.wait_ge(acc[h], 2)
        v.tensor_tensor(T.tb[:, cols[h]], pa[h], slot(h, 3), add).then_inc(acc[h], 1)
        v.wait_ge(acc[h], 3)
        v.wait_ge(S.bb, 2)
        v.tensor_tensor(T.yb[:, cols[h]], T.tb[:, cols[h]], T.pb[:, cols[h]], mult).then_inc([S.yd0, S.yd1][h], 1)
    sy.wait_ge(S.yd0, 1)
    sy.dma_start(T.y[:, cols[0]], T.yb[:, cols[0]]).then_inc(S.st0, 16)
    act.wait_ge(S.yd1, 1)
    act.dma_start(T.y[:, cols[1]], T.yb[:, cols[1]]).then_inc(S.st1, 16)
    g.wait_ge(S.lsem, 3 * fed)
    sy.wait_ge(S.st0, 16)
    act.wait_ge(S.st1, 16)
